import numpy as np
import ml_dtypes


def mxq(x, axis, fmt="e4m3"):
    dtype, down = {"e4m3": (ml_dtypes.float8_e4m3fn, 7), "e5m2": (ml_dtypes.float8_e5m2, 14)}[fmt]
    v = np.moveaxis(np.asarray(x, np.float32).astype(ml_dtypes.bfloat16).astype(np.float64), axis, -1)
    blocks = v.reshape(v.shape[:-1] + (-1, 32))
    amax = np.abs(blocks).max(-1, keepdims=True)
    byte = np.maximum(np.where(amax > 0, np.frexp(amax)[1] - 1 + 127, 0) - down, 1)
    scale = np.exp2(byte - 127.0)
    codes = (blocks / scale).astype(np.float32).astype(dtype).astype(np.float64)
    return np.moveaxis((codes * scale).reshape(v.shape), -1, axis)


WIDE = False


def mx_kscale(k):
    if not WIDE:
        return np.ones(k)
    levels = np.array([10, -10, 5, -5, 0])
    if k % 512:
        return np.exp2(np.random.permutation(np.resize(levels, k // 32))).repeat(32)
    a = np.empty((k // 512, 16))
    for p in range(k // 512):
        a[p, :8] = np.random.permutation(np.resize(levels, 8))
        for g in range(8):
            far = levels[np.abs(levels - a[p, g]) >= 10]
            a[p, g + 8] = far[np.random.randint(len(far))]
    return np.exp2(a.ravel()).repeat(32)


BF16 = ml_dtypes.bfloat16


def bf(x):
    return np.asarray(x, np.float32).astype(BF16)


def f64(x):
    return np.asarray(x).astype(np.float64)


E2M1 = np.array([0.0, 0.5, 1.0, 1.5, 2.0, 3.0, 4.0, 6.0, -0.0, -0.5, -1.0, -1.5, -2.0, -3.0, -4.0, -6.0])


def pack_weight(w, fmt):
    k, n = w.shape
    w = f64(bf(w)).reshape(k // 32, 32, n)
    amax = np.abs(w).max(1)
    if fmt == "e4m3":
        byte = np.frexp(amax)[1] - 1 + 127 - 7
    else:
        mant, ex = np.frexp(amax / 6.0)
        byte = np.where(mant > 0.5, ex, ex - 1) + 127
    byte = np.clip(np.where(amax > 0, byte, 1), 1, 254)
    scaled = (w * np.exp2(127.0 - byte)[:, None, :]).reshape(k, n).astype(np.float32)
    by_word = np.ascontiguousarray(scaled.reshape(k // 512, 128, 4, n).transpose(0, 1, 3, 2))
    if fmt == "e4m3":
        words = by_word.astype(ml_dtypes.float8_e4m3fn).view(np.uint8)
    else:
        c = by_word.astype(ml_dtypes.float4_e2m1fn).view(np.uint8) & 0xF
        words = c[..., 0::2] | (c[..., 1::2] << 4)
    return np.ascontiguousarray(words), np.ascontiguousarray(byte.astype(np.uint8).reshape(k // 512, 16, n))


def unpack_weight(words, scales, fmt):
    g, p, n, _ = words.shape
    if fmt == "e4m3":
        vals = np.ascontiguousarray(words).view(ml_dtypes.float8_e4m3fn).astype(np.float64)
    else:
        nib = np.empty((g, p, n, 4), np.uint8)
        nib[..., 0::2] = words & 0xF
        nib[..., 1::2] = words >> 4
        vals = E2M1[nib]
    vals = vals * np.repeat(np.exp2(scales.astype(np.float64) - 127.0), 8, axis=1)[..., None]
    return vals.transpose(0, 1, 3, 2).reshape(g * 512, n)
def pack4(w):
    words, scales = pack_weight(w, "e2m1")
    return words.reshape(words.shape[0], 128, -1), scales


def unpack4(words, scales):
    return unpack_weight(words.reshape(words.shape[0], 128, -1, 2), scales, "e2m1")


T, D, A = 3072, 1024, 512
CLIP_LO, CLIP_HI = 0.8, 1.2


def draw0():
    s = mx_kscale(D)
    t = mx_kscale(T)
    h = np.random.standard_normal((T, D))
    h_words, h_scales = pack4(h / np.sqrt(T) / t[:, None])
    advantage = np.random.standard_normal(T)
    ratio = np.exp(0.3 * np.random.standard_normal(T))
    return {"x": bf(h * s),
            "w": bf(np.random.standard_normal((D, A)) / np.sqrt(D) / s[:, None]),
            "action": bf(np.random.random((T, A)) < 0.5),
            "weight": bf(advantage * np.clip(ratio, CLIP_LO, CLIP_HI) * t),
            "h_words": h_words,
            "h_scales": h_scales}


def core(x, w, action, weight, h_words, h_scales):
    z = mxq(f64(x), 1, "e4m3") @ mxq(f64(w), 0, "e4m3")
    prob = 1.0 / (1.0 + np.exp(-z))
    g = f64(weight)[:, None] * (prob - f64(action))
    hid = unpack4(h_words, h_scales)
    return hid.T @ mxq(g, 0, "e4m3")


def e4m3fn_bytes(y):
    return np.clip(np.asarray(y, np.float64), -448.0, 448.0).astype(np.float32).astype(ml_dtypes.float8_e4m3fn).view(np.uint8)


def e4m3fn_values(b):
    return np.asarray(b, np.uint8).view(ml_dtypes.float8_e4m3fn).astype(np.float64)


def setup_inputs():
    d = draw0()
    x0 = np.asarray(d['x']).astype(np.float64)
    s = (np.max(np.abs(x0), axis=(0,), keepdims=True) / 448.0).astype(np.float32)
    out = {}
    for k, v in d.items():
        if k == 'x':
            out['x_bytes'] = e4m3fn_bytes(x0 / s.astype(np.float64))
            out['x_scale'] = s
        else:
            out[k] = v
    return out


def reference(x_bytes, x_scale, w, action, weight, h_words, h_scales):
    return core(e4m3fn_values(x_bytes) * x_scale.astype(np.float64), w, action, weight, h_words, h_scales)

@@ -1,0 +1,305 @@
+from contextlib import ExitStack
+
+import concourse.mybir as mybir
+from concourse.masks import make_identity
+
+T, D, A = 3072, 1024, 512
+FLOPS = 2 * T * D * A * 2
+
+F32 = mybir.dt.float32
+BF16 = mybir.dt.bfloat16
+I32 = mybir.dt.int32
+U32 = mybir.dt.uint32
+U8 = mybir.dt.uint8
+FP8 = mybir.dt.float8_e4m3fn
+FP8X4 = mybir.dt.float8_e4m3fn_x4
+FP4X4 = mybir.dt.float4_e2m1fn_x4
+MULT = mybir.AluOpType.mult
+ADD = mybir.AluOpType.add
+SUB = mybir.AluOpType.subtract
+SIGMOID = mybir.ActivationFunctionType.Sigmoid
+
+P = 128
+K_PASS = 512
+GROUPS = T // K_PASS
+HALVES = 2 * GROUPS
+X_PASSES = D // K_PASS
+M_TILES = D // P
+EARLY = 4
+
+
+def tile_clipped_policy_head_grad_s13_kernel(
+    tc, x_bytes, x_scale, w, action, weight, h_words, h_scales, out
+):
+    nc = tc.nc
+    with ExitStack() as ctx:
+        keep = ctx.enter_context(tc.tile_pool(name="keep", bufs=1))
+        three = ctx.enter_context(tc.tile_pool(name="three", bufs=3))
+        four = ctx.enter_context(tc.tile_pool(name="four", bufs=4))
+        two = ctx.enter_context(tc.tile_pool(name="two", bufs=2))
+        psum_t = ctx.enter_context(tc.psum_pool(name="psum_t", bufs=2))
+        psum_z = ctx.enter_context(tc.psum_pool(name="psum_z", bufs=2))
+        psum_o = ctx.enter_context(tc.psum_pool(name="psum_o", bufs=1))
+        ctx.enter_context(tc.manual_schedule())
+
+        x_raw = [keep.tile([P, 4 * D], U8, align_bytes=64, name=f"x_raw{g}") for g in range(GROUPS)]
+        act = [keep.tile([P, 4, A], BF16, align_bytes=64, name=f"act{g}") for g in range(GROUPS)]
+        hw = [keep.tile([P, 2 * D], U8, align_bytes=64, name=f"hw{g}") for g in range(GROUPS)]
+        w_raw = [keep.tile([P, 4, A], BF16, align_bytes=64, name=f"w_raw{c}") for c in range(X_PASSES)]
+        w_int = [keep.tile([P, A, 4], BF16, align_bytes=64, name=f"w_int{c}") for c in range(X_PASSES)]
+        w_codes = [keep.tile([P, A], U32, align_bytes=64, name=f"w_codes{c}") for c in range(X_PASSES)]
+        w_scales = [keep.tile([P, A], U8, align_bytes=64, name=f"w_scales{c}") for c in range(X_PASSES)]
+        g_codes = [keep.tile([P, A], U32, align_bytes=64, name=f"g_codes{g}") for g in range(GROUPS)]
+        g_scales = [keep.tile([P, A], U8, align_bytes=64, name=f"g_scales{g}") for g in range(GROUPS)]
+        hs = keep.tile([P, GROUPS, D // 4], I32, align_bytes=64, name="hs")
+        xs = keep.tile([P, X_PASSES, 2, 2], F32, align_bytes=64, name="xs")
+        wt_raw = keep.tile([P, GROUPS, 4], BF16, align_bytes=64, name="wt_raw")
+        wt = keep.tile([P, GROUPS, 4], F32, align_bytes=64, name="wt")
+        ident = keep.tile([P, P], F32, align_bytes=64, name="ident")
+        warm = keep.tile([P, 1], F32, align_bytes=64, name="warm")
+
+        def load_x(g, lo, hi):
+            src = x_bytes[g * K_PASS : (g + 1) * K_PASS, :].rearrange("(p t) k -> p (t k)", t=4)
+            nc.sync.dma_start(out=x_raw[g][:, lo * D : hi * D], in_=src[:, lo * D : hi * D])
+
+        def load_w(c):
+            nc.sync.dma_start(
+                out=w_raw[c][:], in_=w[c * K_PASS : (c + 1) * K_PASS, :].rearrange("(p j) n -> p j n", j=4)
+            )
+
+        def load_act(g):
+            nc.sync.dma_start(
+                out=act[g][:], in_=action[g * K_PASS : (g + 1) * K_PASS, :].rearrange("(p t) a -> p t a", t=4)
+            )
+
+        def load_h(g):
+            nc.sync.dma_start(out=hw[g][:], in_=h_words[g])
+
+        nc.vector.memset(warm[:], 0.0)
+        nc.scalar.activation(out=warm[:], in_=warm[:], func=SIGMOID)
+        make_identity(nc, ident[:])
+        nc.gpsimd.memset(hs[:], 0)
+
+        load_x(0, 0, 2)
+        load_w(0)
+        nc.sync.dma_start(
+            out=xs[:].rearrange("p c u e -> p c (u e)"),
+            in_=x_scale.rearrange("o (c p t) -> p (o c) t", p=P, t=4),
+        )
+        load_w(1)
+        load_x(0, 2, 4)
+        nc.sync.dma_start(out=wt_raw[:], in_=weight.rearrange("(g p t) -> p g t", p=P, t=4))
+        load_x(1, 0, 4)
+        load_act(0)
+        load_x(2, 0, 4)
+        load_act(1)
+        scales_src = h_scales.bitcast(I32).rearrange("g (q r) n -> r q g n", r=4)
+        for r in range(4):
+            nc.sync.dma_start(out=hs[r:P:32, :, :], in_=scales_src[r])
+        load_h(0)
+        load_x(3, 0, 4)
+        load_act(2)
+        load_h(1)
+        for g in range(3, GROUPS):
+            if g + 1 < GROUPS:
+                load_x(g + 1, 0, 4)
+            load_act(g)
+            load_h(g - 1)
+        load_h(GROUPS - 1)
+
+        cast = {}
+        banks = {}
+        xg = {}
+        x_codes = {}
+        x_scales = {}
+        z = {}
+        sig = {}
+        aw = {}
+        gp = {}
+        gi = {}
+
+        def do_cast(h, split):
+            if h >= HALVES:
+                return
+            g, lo = h // 2, 2 * (h % 2)
+            cast[h] = three.tile([P, 2 * D], BF16, align_bytes=64, name="cast")
+            step = 2 // split
+            for i in range(split):
+                cols = slice(i * step * D, (i + 1) * step * D)
+                raw = slice((lo + i * step) * D, (lo + (i + 1) * step) * D)
+                nc.scalar.copy(out=cast[h][:, cols], in_=x_raw[g][:, raw].bitcast(FP8))
+
+        def do_transposes(h, c):
+            if h >= HALVES:
+                return
+            bank = psum_t.tile([P, 2, 2 * P], F32, name="bank")
+            banks[h, c] = bank
+            for i in range(2):
+                words = cast[h][:, i * D : (i + 1) * D].bitcast(F32)
+                for u in range(2):
+                    nc.tensor.transpose(
+                        bank[:, u, i * P : (i + 1) * P], words[:, 256 * c + u : 256 * (c + 1) : 2], ident[:]
+                    )
+
+        def do_scale(h, c):
+            if c == 0:
+                xg[h] = three.tile([P, X_PASSES, 2 * P, 2, 2], BF16, align_bytes=64, name="xg")
+            nc.vector.tensor_tensor(
+                out=xg[h][:, c],
+                in0=banks[h, c][:].bitcast(BF16).rearrange("p u (r e) -> p r u e", e=2),
+                in1=xs[:, c].unsqueeze(1).to_broadcast([P, 2 * P, 2, 2]),
+                op=MULT,
+            )
+
+        def do_quant_x(h):
+            x_codes[h] = four.tile([P, X_PASSES, 2 * P], U32, align_bytes=64, name="x_codes")
+            x_scales[h] = four.tile([P, X_PASSES, 2 * P], U8, align_bytes=64, name="x_scales")
+            nc.vector.quantize_mx(
+                out=x_codes[h][:].rearrange("p c r -> p (c r)").bitcast(FP8X4),
+                scales=x_scales[h][:].rearrange("p c r -> p (c r)"),
+                in_=xg[h][:].rearrange("p c r u e -> p (c r u e)"),
+            )
+
+        def do_z(h, i):
+            zt = psum_z.tile([P, A], F32, name="zt")
+            z[h, i] = zt
+            for c in range(X_PASSES):
+                nc.tensor.matmul_mx(
+                    out=zt[:],
+                    lhsT=x_codes[h][:, c, i * P : (i + 1) * P].bitcast(FP8X4),
+                    lhsT_scale=x_scales[h][:, c, i * P : (i + 1) * P],
+                    rhs=w_codes[c][:].bitcast(FP8X4),
+                    rhs_scale=w_scales[c][:],
+                    start=(c == 0),
+                    stop=(c == X_PASSES - 1),
+                )
+
+        def do_sigmoid(h, i):
+            if i == 0:
+                sig[h] = three.tile([P, 2, A], F32, align_bytes=64, name="sig")
+            nc.scalar.activation(out=sig[h][:, i, :], in_=z[h, i][:], func=SIGMOID)
+
+        def do_aw(g):
+            aw[g] = three.tile([P, 4, A], F32, align_bytes=64, name="aw")
+            for t in range(4):
+                nc.gpsimd.tensor_scalar(
+                    out=aw[g][:, t, :], in0=act[g][:, t, :], scalar1=wt[:, g, t : t + 1], scalar2=0.0,
+                    op0=MULT, op1=ADD,
+                )
+
+        def do_residual(h, i):
+            g, t = h // 2, 2 * (h % 2) + i
+            if t == 0:
+                gp[g] = two.tile([P, 4, A], BF16, align_bytes=64, name="gp")
+            nc.vector.scalar_tensor_tensor(
+                out=gp[g][:, t, :], in0=sig[h][:, i, :], scalar=wt[:, g, t : t + 1], in1=aw[g][:, t, :],
+                op0=MULT, op1=SUB,
+            )
+
+        def do_interleave(g, lo, hi, vector):
+            if lo == 0:
+                gi[g] = two.tile([P, A, 4], BF16, align_bytes=64, name="gi")
+            dst = gi[g][:, lo:hi, :]
+            src = gp[g][:, :, lo:hi].rearrange("p t a -> p a t")
+            if vector:
+                nc.vector.tensor_copy(out=dst, in_=src)
+            else:
+                nc.scalar.copy(out=dst, in_=src)
+
+        def do_quant_g(g, lo, hi):
+            nc.vector.quantize_mx(
+                out=g_codes[g][:, lo:hi].bitcast(FP8X4),
+                scales=g_scales[g][:, lo:hi],
+                in_=gi[g][:, lo:hi, :].rearrange("p a t -> p (a t)"),
+            )
+
+        def do_out(acc, m, g):
+            nc.tensor.matmul_mx(
+                out=acc[:],
+                lhsT=hw[g][:, 2 * P * m : 2 * P * (m + 1)].bitcast(FP4X4),
+                lhsT_scale=hs[:, g, 32 * m : 32 * (m + 1)].bitcast(U8),
+                rhs=g_codes[g][:].bitcast(FP8X4),
+                rhs_scale=g_scales[g][:],
+                start=(g == 0),
+                stop=(g == GROUPS - 1),
+            )
+
+        def do_w_interleave(c):
+            nc.vector.tensor_copy(out=w_int[c][:], in_=w_raw[c][:].rearrange("p j n -> p n j"))
+
+        def do_quant_w(c):
+            nc.vector.quantize_mx(
+                out=w_codes[c][:].bitcast(FP8X4), scales=w_scales[c][:],
+                in_=w_int[c][:].rearrange("p n j -> p (n j)"),
+            )
+
+        accs = [psum_o.tile([P, A], F32, name=f"acc{m}") for m in range(EARLY)]
+
+        do_cast(0, 2)
+        do_cast(1, 1)
+        do_w_interleave(0)
+        do_transposes(0, 0)
+        do_transposes(0, 1)
+        do_w_interleave(1)
+
+        for h in range(HALVES):
+            if h >= 1:
+                for i in range(2):
+                    do_z(h - 1, i)
+                    do_sigmoid(h - 1, i)
+            if h % 2 == 1 and h >= 3:
+                do_interleave((h - 3) // 2, 0, A, False)
+            do_cast(h + 2, 1)
+            do_scale(h, 0)
+            if h == 0:
+                do_quant_w(0)
+            do_transposes(h + 1, 0)
+            do_scale(h, 1)
+            if h == 0:
+                do_quant_w(1)
+                nc.vector.tensor_copy(out=wt[:], in_=wt_raw[:])
+            do_transposes(h + 1, 1)
+            if h % 2 == 0 and h >= 4:
+                do_quant_g((h - 4) // 2, 0, A)
+            if h % 2 == 0:
+                do_aw(h // 2)
+            if h >= 4:
+                g = (h - 4) // 2
+                for m in (range(2) if h % 2 == 0 else range(2, EARLY)):
+                    do_out(accs[m], m, g)
+            if h >= 1:
+                for i in range(2):
+                    do_residual(h - 1, i)
+            do_quant_x(h)
+
+        last = GROUPS - 1
+        accs.append(psum_t.tile([P, A], F32, name="bank"))
+        accs.append(psum_t.tile([P, A], F32, name="bank"))
+        for m in range(EARLY, EARLY + 2):
+            for g in range(last - 1):
+                do_out(accs[m], m, g)
+        for i in range(2):
+            do_z(HALVES - 1, i)
+            do_sigmoid(HALVES - 1, i)
+        do_quant_g(last - 1, 0, A)
+        for m in range(EARLY + 2):
+            do_out(accs[m], m, last - 1)
+        for i in range(2):
+            do_residual(HALVES - 1, i)
+        accs.append(psum_z.tile([P, A], F32, name="zt"))
+        accs.append(psum_z.tile([P, A], F32, name="zt"))
+        for m in range(EARLY + 2, M_TILES):
+            for g in range(last):
+                do_out(accs[m], m, g)
+        do_interleave(last, 0, 256, True)
+        do_interleave(last, 256, A, False)
+        do_quant_g(last, 0, 256)
+        do_quant_g(last, 256, A)
+        for m in range(M_TILES):
+            do_out(accs[m], m, last)
+            res = keep.tile([P, A], F32, align_bytes=64, name=f"res{m}")
+            if m % 2 == 0:
+                nc.vector.tensor_copy(out=res[:], in_=accs[m][:])
+            else:
+                nc.scalar.copy(out=res[:], in_=accs[m][:])
+            nc.sync.dma_start(out=out[m * P : (m + 1) * P, :], in_=res[:])

@@ -26,6 +26,7 @@ HALVES = 2 * GROUPS
 X_PASSES = D // K_PASS
 M_TILES = D // P
 EARLY = 4
+POOL_TILES = tuple((h, 0) for h in range(0, 12, 2))
 
 
 def tile_clipped_policy_head_grad_s13_kernel(
@@ -176,23 +177,43 @@ def tile_clipped_policy_head_grad_s13_kernel(
 
         def do_sigmoid(h, i):
             if i == 0:
-                sig[h] = three.tile([P, 2, A], F32, align_bytes=64, name="sig")
+                sig[h] = four.tile([P, 2, A], F32, align_bytes=64, name="sig")
             nc.scalar.activation(out=sig[h][:, i, :], in_=z[h, i][:], func=SIGMOID)
 
-        def do_aw(g):
-            aw[g] = three.tile([P, 4, A], F32, align_bytes=64, name="aw")
-            for t in range(4):
+        def do_aw(h):
+            if h >= HALVES:
+                return
+            g = h // 2
+            aw[h] = three.tile([P, 2, A], F32, align_bytes=64, name="aw")
+            for i in range(2):
+                t = 2 * (h % 2) + i
+                if (h, i) in POOL_TILES:
+                    continue
                 nc.gpsimd.tensor_scalar(
-                    out=aw[g][:, t, :], in0=act[g][:, t, :], scalar1=wt[:, g, t : t + 1], scalar2=0.0,
+                    out=aw[h][:, i, :], in0=act[g][:, t, :], scalar1=wt[:, g, t : t + 1], scalar2=0.0,
                     op0=MULT, op1=ADD,
                 )
 
+        def do_residual_pool(h):
+            for i in range(2):
+                if (h, i) in POOL_TILES:
+                    g, t = h // 2, 2 * (h % 2) + i
+                    if t == 0:
+                        gp[g] = two.tile([P, 4, A], BF16, align_bytes=64, name="gp")
+                    nc.gpsimd.tensor_tensor(out=aw[h][:, i, :], in0=sig[h][:, i, :], in1=act[g][:, t, :], op=SUB)
+                    nc.gpsimd.tensor_scalar(
+                        out=gp[g][:, t, :], in0=aw[h][:, i, :], scalar1=wt[:, g, t : t + 1], scalar2=1.0,
+                        op0=MULT, op1=MULT,
+                    )
+
         def do_residual(h, i):
             g, t = h // 2, 2 * (h % 2) + i
+            if (h, i) in POOL_TILES:
+                return
             if t == 0:
                 gp[g] = two.tile([P, 4, A], BF16, align_bytes=64, name="gp")
             nc.vector.scalar_tensor_tensor(
-                out=gp[g][:, t, :], in0=sig[h][:, i, :], scalar=wt[:, g, t : t + 1], in1=aw[g][:, t, :],
+                out=gp[g][:, t, :], in0=sig[h][:, i, :], scalar=wt[:, g, t : t + 1], in1=aw[h][:, i, :],
                 op0=MULT, op1=SUB,
             )
 
@@ -224,8 +245,11 @@ def tile_clipped_policy_head_grad_s13_kernel(
                 stop=(g == GROUPS - 1),
             )
 
-        def do_w_interleave(c):
-            nc.vector.tensor_copy(out=w_int[c][:], in_=w_raw[c][:].rearrange("p j n -> p n j"))
+        def do_w_interleave(c, vector):
+            if vector:
+                nc.vector.tensor_copy(out=w_int[c][:], in_=w_raw[c][:].rearrange("p j n -> p n j"))
+            else:
+                nc.scalar.copy(out=w_int[c][:], in_=w_raw[c][:].rearrange("p j n -> p n j"))
 
         def do_quant_w(c):
             nc.vector.quantize_mx(
@@ -237,65 +261,82 @@ def tile_clipped_policy_head_grad_s13_kernel(
 
         do_cast(0, 2)
         do_cast(1, 1)
-        do_w_interleave(0)
+        do_w_interleave(0, True)
         do_transposes(0, 0)
         do_transposes(0, 1)
-        do_w_interleave(1)
+        do_w_interleave(1, False)
 
         for h in range(HALVES):
             if h >= 1:
                 for i in range(2):
                     do_z(h - 1, i)
                     do_sigmoid(h - 1, i)
-            if h % 2 == 1 and h >= 3:
-                do_interleave((h - 3) // 2, 0, A, False)
+            if h % 2 == 0 and h >= 4:
+                do_interleave((h - 4) // 2, 0, A, False)
             do_cast(h + 2, 1)
             do_scale(h, 0)
             if h == 0:
                 do_quant_w(0)
             do_transposes(h + 1, 0)
+            if h >= 1:
+                do_aw(h - 1)
+            if h >= 2:
+                do_residual_pool(h - 2)
             do_scale(h, 1)
             if h == 0:
-                do_quant_w(1)
                 nc.vector.tensor_copy(out=wt[:], in_=wt_raw[:])
             do_transposes(h + 1, 1)
-            if h % 2 == 0 and h >= 4:
-                do_quant_g((h - 4) // 2, 0, A)
-            if h % 2 == 0:
-                do_aw(h // 2)
-            if h >= 4:
-                g = (h - 4) // 2
-                for m in (range(2) if h % 2 == 0 else range(2, EARLY)):
+            if h % 2 == 1 and h >= 5:
+                do_quant_g((h - 5) // 2, 0, A)
+            if h >= 5:
+                g = (h - 5) // 2
+                for m in (range(2) if h % 2 == 1 else range(2, EARLY)):
                     do_out(accs[m], m, g)
-            if h >= 1:
+            if h >= 2 and h < HALVES - 1:
                 for i in range(2):
-                    do_residual(h - 1, i)
+                    do_residual(h - 2, i)
+            if h == HALVES - 1:
+                do_residual(h - 2, 0)
             do_quant_x(h)
+            if h == 0:
+                do_quant_w(1)
 
         last = GROUPS - 1
+        for m in range(2, EARLY):
+            do_out(accs[m], m, last - 2)
         accs.append(psum_t.tile([P, A], F32, name="bank"))
         accs.append(psum_t.tile([P, A], F32, name="bank"))
-        for m in range(EARLY, EARLY + 2):
-            for g in range(last - 1):
-                do_out(accs[m], m, g)
+        do_aw(HALVES - 1)
+        for g in range(last - 1):
+            do_out(accs[EARLY], EARLY, g)
+        do_residual(HALVES - 3, 1)
+        do_residual_pool(HALVES - 2)
         for i in range(2):
             do_z(HALVES - 1, i)
             do_sigmoid(HALVES - 1, i)
-        do_quant_g(last - 1, 0, A)
-        for m in range(EARLY + 2):
-            do_out(accs[m], m, last - 1)
         for i in range(2):
-            do_residual(HALVES - 1, i)
+            do_residual(HALVES - 2, i)
+        for g in range(last - 1):
+            do_out(accs[EARLY + 1], EARLY + 1, g)
         accs.append(psum_z.tile([P, A], F32, name="zt"))
         accs.append(psum_z.tile([P, A], F32, name="zt"))
-        for m in range(EARLY + 2, M_TILES):
-            for g in range(last):
-                do_out(accs[m], m, g)
+        for g in range(last - 1):
+            do_out(accs[EARLY + 2], EARLY + 2, g)
+        do_interleave(last - 1, 0, 256, False)
+        do_residual(HALVES - 1, 0)
+        do_interleave(last - 1, 256, A, True)
+        do_residual(HALVES - 1, 1)
+        do_quant_g(last - 1, 0, A)
         do_interleave(last, 0, 256, True)
         do_interleave(last, 256, A, False)
+        for m in range(EARLY + 3):
+            do_out(accs[m], m, last - 1)
         do_quant_g(last, 0, 256)
         do_quant_g(last, 256, A)
         for m in range(M_TILES):
+            if m == EARLY + 3:
+                for g in range(last):
+                    do_out(accs[m], m, g)
             do_out(accs[m], m, last)
             res = keep.tile([P, A], F32, align_bytes=64, name=f"res{m}")
             if m % 2 == 0:

from contextlib import ExitStack

import concourse.mybir as mybir
from concourse.masks import make_identity

T, D, A = 3072, 1024, 512
FLOPS = 2 * T * D * A * 2

F32 = mybir.dt.float32
BF16 = mybir.dt.bfloat16
I32 = mybir.dt.int32
U32 = mybir.dt.uint32
U8 = mybir.dt.uint8
FP8 = mybir.dt.float8_e4m3fn
FP8X4 = mybir.dt.float8_e4m3fn_x4
FP4X4 = mybir.dt.float4_e2m1fn_x4
MULT = mybir.AluOpType.mult
ADD = mybir.AluOpType.add
SUB = mybir.AluOpType.subtract
SIGMOID = mybir.ActivationFunctionType.Sigmoid

P = 128
K_PASS = 512
GROUPS = T // K_PASS
HALVES = 2 * GROUPS
X_PASSES = D // K_PASS
M_TILES = D // P
EARLY = 4
POOL_TILES = tuple((h, 0) for h in range(0, 12, 2))


def tile_clipped_policy_head_grad_s13_kernel(
    tc, x_bytes, x_scale, w, action, weight, h_words, h_scales, out
):
    nc = tc.nc
    with ExitStack() as ctx:
        keep = ctx.enter_context(tc.tile_pool(name="keep", bufs=1))
        three = ctx.enter_context(tc.tile_pool(name="three", bufs=3))
        four = ctx.enter_context(tc.tile_pool(name="four", bufs=4))
        two = ctx.enter_context(tc.tile_pool(name="two", bufs=2))
        psum_t = ctx.enter_context(tc.psum_pool(name="psum_t", bufs=2))
        psum_z = ctx.enter_context(tc.psum_pool(name="psum_z", bufs=2))
        psum_o = ctx.enter_context(tc.psum_pool(name="psum_o", bufs=1))
        ctx.enter_context(tc.manual_schedule())

        x_raw = [keep.tile([P, 4 * D], U8, align_bytes=64, name=f"x_raw{g}") for g in range(GROUPS)]
        act = [keep.tile([P, 4, A], BF16, align_bytes=64, name=f"act{g}") for g in range(GROUPS)]
        hw = [keep.tile([P, 2 * D], U8, align_bytes=64, name=f"hw{g}") for g in range(GROUPS)]
        w_raw = [keep.tile([P, 4, A], BF16, align_bytes=64, name=f"w_raw{c}") for c in range(X_PASSES)]
        w_int = [keep.tile([P, A, 4], BF16, align_bytes=64, name=f"w_int{c}") for c in range(X_PASSES)]
        w_codes = [keep.tile([P, A], U32, align_bytes=64, name=f"w_codes{c}") for c in range(X_PASSES)]
        w_scales = [keep.tile([P, A], U8, align_bytes=64, name=f"w_scales{c}") for c in range(X_PASSES)]
        g_codes = [keep.tile([P, A], U32, align_bytes=64, name=f"g_codes{g}") for g in range(GROUPS)]
        g_scales = [keep.tile([P, A], U8, align_bytes=64, name=f"g_scales{g}") for g in range(GROUPS)]
        hs = keep.tile([P, GROUPS, D // 4], I32, align_bytes=64, name="hs")
        xs = keep.tile([P, X_PASSES, 2, 2], F32, align_bytes=64, name="xs")
        wt_raw = keep.tile([P, GROUPS, 4], BF16, align_bytes=64, name="wt_raw")
        wt = keep.tile([P, GROUPS, 4], F32, align_bytes=64, name="wt")
        ident = keep.tile([P, P], F32, align_bytes=64, name="ident")
        warm = keep.tile([P, 1], F32, align_bytes=64, name="warm")

        def load_x(g, lo, hi):
            src = x_bytes[g * K_PASS : (g + 1) * K_PASS, :].rearrange("(p t) k -> p (t k)", t=4)
            nc.sync.dma_start(out=x_raw[g][:, lo * D : hi * D], in_=src[:, lo * D : hi * D])

        def load_w(c):
            nc.sync.dma_start(
                out=w_raw[c][:], in_=w[c * K_PASS : (c + 1) * K_PASS, :].rearrange("(p j) n -> p j n", j=4)
            )

        def load_act(g):
            nc.sync.dma_start(
                out=act[g][:], in_=action[g * K_PASS : (g + 1) * K_PASS, :].rearrange("(p t) a -> p t a", t=4)
            )

        def load_h(g):
            nc.sync.dma_start(out=hw[g][:], in_=h_words[g])

        nc.vector.memset(warm[:], 0.0)
        nc.scalar.activation(out=warm[:], in_=warm[:], func=SIGMOID)
        make_identity(nc, ident[:])
        nc.gpsimd.memset(hs[:], 0)

        load_x(0, 0, 2)
        load_w(0)
        nc.sync.dma_start(
            out=xs[:].rearrange("p c u e -> p c (u e)"),
            in_=x_scale.rearrange("o (c p t) -> p (o c) t", p=P, t=4),
        )
        load_w(1)
        load_x(0, 2, 4)
        nc.sync.dma_start(out=wt_raw[:], in_=weight.rearrange("(g p t) -> p g t", p=P, t=4))
        load_x(1, 0, 4)
        load_act(0)
        load_x(2, 0, 4)
        load_act(1)
        scales_src = h_scales.bitcast(I32).rearrange("g (q r) n -> r q g n", r=4)
        for r in range(4):
            nc.sync.dma_start(out=hs[r:P:32, :, :], in_=scales_src[r])
        load_h(0)
        load_x(3, 0, 4)
        load_act(2)
        load_h(1)
        for g in range(3, GROUPS):
            if g + 1 < GROUPS:
                load_x(g + 1, 0, 4)
            load_act(g)
            load_h(g - 1)
        load_h(GROUPS - 1)

        cast = {}
        banks = {}
        xg = {}
        x_codes = {}
        x_scales = {}
        z = {}
        sig = {}
        aw = {}
        gp = {}
        gi = {}

        def do_cast(h, split):
            if h >= HALVES:
                return
            g, lo = h // 2, 2 * (h % 2)
            cast[h] = three.tile([P, 2 * D], BF16, align_bytes=64, name="cast")
            step = 2 // split
            for i in range(split):
                cols = slice(i * step * D, (i + 1) * step * D)
                raw = slice((lo + i * step) * D, (lo + (i + 1) * step) * D)
                nc.scalar.copy(out=cast[h][:, cols], in_=x_raw[g][:, raw].bitcast(FP8))

        def do_transposes(h, c):
            if h >= HALVES:
                return
            bank = psum_t.tile([P, 2, 2 * P], F32, name="bank")
            banks[h, c] = bank
            for i in range(2):
                words = cast[h][:, i * D : (i + 1) * D].bitcast(F32)
                for u in range(2):
                    nc.tensor.transpose(
                        bank[:, u, i * P : (i + 1) * P], words[:, 256 * c + u : 256 * (c + 1) : 2], ident[:]
                    )

        def do_scale(h, c):
            if c == 0:
                xg[h] = three.tile([P, X_PASSES, 2 * P, 2, 2], BF16, align_bytes=64, name="xg")
            nc.vector.tensor_tensor(
                out=xg[h][:, c],
                in0=banks[h, c][:].bitcast(BF16).rearrange("p u (r e) -> p r u e", e=2),
                in1=xs[:, c].unsqueeze(1).to_broadcast([P, 2 * P, 2, 2]),
                op=MULT,
            )

        def do_quant_x(h):
            x_codes[h] = four.tile([P, X_PASSES, 2 * P], U32, align_bytes=64, name="x_codes")
            x_scales[h] = four.tile([P, X_PASSES, 2 * P], U8, align_bytes=64, name="x_scales")
            nc.vector.quantize_mx(
                out=x_codes[h][:].rearrange("p c r -> p (c r)").bitcast(FP8X4),
                scales=x_scales[h][:].rearrange("p c r -> p (c r)"),
                in_=xg[h][:].rearrange("p c r u e -> p (c r u e)"),
            )

        def do_z(h, i):
            zt = psum_z.tile([P, A], F32, name="zt")
            z[h, i] = zt
            for c in range(X_PASSES):
                nc.tensor.matmul_mx(
                    out=zt[:],
                    lhsT=x_codes[h][:, c, i * P : (i + 1) * P].bitcast(FP8X4),
                    lhsT_scale=x_scales[h][:, c, i * P : (i + 1) * P],
                    rhs=w_codes[c][:].bitcast(FP8X4),
                    rhs_scale=w_scales[c][:],
                    start=(c == 0),
                    stop=(c == X_PASSES - 1),
                )

        def do_sigmoid(h, i):
            if i == 0:
                sig[h] = four.tile([P, 2, A], F32, align_bytes=64, name="sig")
            nc.scalar.activation(out=sig[h][:, i, :], in_=z[h, i][:], func=SIGMOID)

        def do_aw(h):
            if h >= HALVES:
                return
            g = h // 2
            aw[h] = three.tile([P, 2, A], F32, align_bytes=64, name="aw")
            for i in range(2):
                t = 2 * (h % 2) + i
                if (h, i) in POOL_TILES:
                    continue
                nc.gpsimd.tensor_scalar(
                    out=aw[h][:, i, :], in0=act[g][:, t, :], scalar1=wt[:, g, t : t + 1], scalar2=0.0,
                    op0=MULT, op1=ADD,
                )

        def do_residual_pool(h):
            for i in range(2):
                if (h, i) in POOL_TILES:
                    g, t = h // 2, 2 * (h % 2) + i
                    if t == 0:
                        gp[g] = two.tile([P, 4, A], BF16, align_bytes=64, name="gp")
                    nc.gpsimd.tensor_tensor(out=aw[h][:, i, :], in0=sig[h][:, i, :], in1=act[g][:, t, :], op=SUB)
                    nc.gpsimd.tensor_scalar(
                        out=gp[g][:, t, :], in0=aw[h][:, i, :], scalar1=wt[:, g, t : t + 1], scalar2=1.0,
                        op0=MULT, op1=MULT,
                    )

        def do_residual(h, i):
            g, t = h // 2, 2 * (h % 2) + i
            if (h, i) in POOL_TILES:
                return
            if t == 0:
                gp[g] = two.tile([P, 4, A], BF16, align_bytes=64, name="gp")
            nc.vector.scalar_tensor_tensor(
                out=gp[g][:, t, :], in0=sig[h][:, i, :], scalar=wt[:, g, t : t + 1], in1=aw[h][:, i, :],
                op0=MULT, op1=SUB,
            )

        def do_interleave(g, lo, hi, vector):
            if lo == 0:
                gi[g] = two.tile([P, A, 4], BF16, align_bytes=64, name="gi")
            dst = gi[g][:, lo:hi, :]
            src = gp[g][:, :, lo:hi].rearrange("p t a -> p a t")
            if vector:
                nc.vector.tensor_copy(out=dst, in_=src)
            else:
                nc.scalar.copy(out=dst, in_=src)

        def do_quant_g(g, lo, hi):
            nc.vector.quantize_mx(
                out=g_codes[g][:, lo:hi].bitcast(FP8X4),
                scales=g_scales[g][:, lo:hi],
                in_=gi[g][:, lo:hi, :].rearrange("p a t -> p (a t)"),
            )

        def do_out(acc, m, g):
            nc.tensor.matmul_mx(
                out=acc[:],
                lhsT=hw[g][:, 2 * P * m : 2 * P * (m + 1)].bitcast(FP4X4),
                lhsT_scale=hs[:, g, 32 * m : 32 * (m + 1)].bitcast(U8),
                rhs=g_codes[g][:].bitcast(FP8X4),
                rhs_scale=g_scales[g][:],
                start=(g == 0),
                stop=(g == GROUPS - 1),
            )

        def do_w_interleave(c, vector):
            if vector:
                nc.vector.tensor_copy(out=w_int[c][:], in_=w_raw[c][:].rearrange("p j n -> p n j"))
            else:
                nc.scalar.copy(out=w_int[c][:], in_=w_raw[c][:].rearrange("p j n -> p n j"))

        def do_quant_w(c):
            nc.vector.quantize_mx(
                out=w_codes[c][:].bitcast(FP8X4), scales=w_scales[c][:],
                in_=w_int[c][:].rearrange("p n j -> p (n j)"),
            )

        accs = [psum_o.tile([P, A], F32, name=f"acc{m}") for m in range(EARLY)]

        do_cast(0, 2)
        do_cast(1, 1)
        do_w_interleave(0, True)
        do_transposes(0, 0)
        do_transposes(0, 1)
        do_w_interleave(1, False)

        for h in range(HALVES):
            if h >= 1:
                for i in range(2):
                    do_z(h - 1, i)
                    do_sigmoid(h - 1, i)
            if h % 2 == 0 and h >= 4:
                do_interleave((h - 4) // 2, 0, A, False)
            do_cast(h + 2, 1)
            do_scale(h, 0)
            if h == 0:
                do_quant_w(0)
            do_transposes(h + 1, 0)
            if h >= 1:
                do_aw(h - 1)
            if h >= 2:
                do_residual_pool(h - 2)
            do_scale(h, 1)
            if h == 0:
                nc.vector.tensor_copy(out=wt[:], in_=wt_raw[:])
            do_transposes(h + 1, 1)
            if h % 2 == 1 and h >= 5:
                do_quant_g((h - 5) // 2, 0, A)
            if h >= 5:
                g = (h - 5) // 2
                for m in (range(2) if h % 2 == 1 else range(2, EARLY)):
                    do_out(accs[m], m, g)
            if h >= 2 and h < HALVES - 1:
                for i in range(2):
                    do_residual(h - 2, i)
            if h == HALVES - 1:
                do_residual(h - 2, 0)
            do_quant_x(h)
            if h == 0:
                do_quant_w(1)

        last = GROUPS - 1
        for m in range(2, EARLY):
            do_out(accs[m], m, last - 2)
        accs.append(psum_t.tile([P, A], F32, name="bank"))
        accs.append(psum_t.tile([P, A], F32, name="bank"))
        do_aw(HALVES - 1)
        for g in range(last - 1):
            do_out(accs[EARLY], EARLY, g)
        do_residual(HALVES - 3, 1)
        do_residual_pool(HALVES - 2)
        for i in range(2):
            do_z(HALVES - 1, i)
            do_sigmoid(HALVES - 1, i)
        for i in range(2):
            do_residual(HALVES - 2, i)
        for g in range(last - 1):
            do_out(accs[EARLY + 1], EARLY + 1, g)
        accs.append(psum_z.tile([P, A], F32, name="zt"))
        accs.append(psum_z.tile([P, A], F32, name="zt"))
        for g in range(last - 1):
            do_out(accs[EARLY + 2], EARLY + 2, g)
        do_interleave(last - 1, 0, 256, False)
        do_residual(HALVES - 1, 0)
        do_interleave(last - 1, 256, A, True)
        do_residual(HALVES - 1, 1)
        do_quant_g(last - 1, 0, A)
        do_interleave(last, 0, 256, True)
        do_interleave(last, 256, A, False)
        for m in range(EARLY + 3):
            do_out(accs[m], m, last - 1)
        do_quant_g(last, 0, 256)
        do_quant_g(last, 256, A)
        for m in range(M_TILES):
            if m == EARLY + 3:
                for g in range(last):
                    do_out(accs[m], m, g)
            do_out(accs[m], m, last)
            res = keep.tile([P, A], F32, align_bytes=64, name=f"res{m}")
            if m % 2 == 0:
                nc.vector.tensor_copy(out=res[:], in_=accs[m][:])
            else:
                nc.scalar.copy(out=res[:], in_=accs[m][:])
            nc.sync.dma_start(out=out[m * P : (m + 1) * P, :], in_=res[:])
